import numpy as np
import ml_dtypes


def mxq(x, axis, fmt="e4m3"):
    dtype, down = {"e4m3": (ml_dtypes.float8_e4m3fn, 7), "e5m2": (ml_dtypes.float8_e5m2, 14)}[fmt]
    v = np.moveaxis(np.asarray(x, np.float32).astype(ml_dtypes.bfloat16).astype(np.float64), axis, -1)
    blocks = v.reshape(v.shape[:-1] + (-1, 32))
    amax = np.abs(blocks).max(-1, keepdims=True)
    byte = np.maximum(np.where(amax > 0, np.frexp(amax)[1] - 1 + 127, 0) - down, 1)
    scale = np.exp2(byte - 127.0)
    codes = (blocks / scale).astype(np.float32).astype(dtype).astype(np.float64)
    return np.moveaxis((codes * scale).reshape(v.shape), -1, axis)


WIDE = False


def mx_kscale(k):
    if not WIDE:
        return np.ones(k)
    levels = np.array([10, -10, 5, -5, 0])
    if k % 512:
        return np.exp2(np.random.permutation(np.resize(levels, k // 32))).repeat(32)
    a = np.empty((k // 512, 16))
    for p in range(k // 512):
        a[p, :8] = np.random.permutation(np.resize(levels, 8))
        for g in range(8):
            far = levels[np.abs(levels - a[p, g]) >= 10]
            a[p, g + 8] = far[np.random.randint(len(far))]
    return np.exp2(a.ravel()).repeat(32)


def f64(x):
    return np.asarray(x).astype(np.float64)


def striped(idx):
    return np.tile(idx.reshape(-1, 16).T, (8, 1)).astype(np.uint16)


def unstriped(offs):
    return offs[:16].T.reshape(-1).astype(np.int64)


def striped8(idx):
    return np.concatenate([x.reshape(-1, 16).T for x in idx]).astype(np.uint16)


def runs(offs, k):
    lists = np.stack([offs[16 * r : 16 * r + 16].T.reshape(-1) for r in range(8)]).astype(np.int64)
    return lists[np.arange(k) % 512 // 64]


def pack_weight(w):
    k, n = w.shape
    w = f64(np.asarray(w, np.float32).astype(ml_dtypes.bfloat16)).reshape(k // 32, 32, n)
    amax = np.abs(w).max(1)
    byte = np.clip(np.where(amax > 0, np.frexp(amax)[1] - 1 + 127 - 7, 1), 1, 254)
    scaled = (w * np.exp2(127.0 - byte)[:, None, :]).reshape(k, n).astype(np.float32)
    words = np.ascontiguousarray(scaled.reshape(k // 512, 128, 4, n).transpose(0, 1, 3, 2)).astype(ml_dtypes.float8_e4m3fn).view(np.uint8)
    return words, np.ascontiguousarray(byte.astype(np.uint8).reshape(k // 512, 16, n))


def unpack_weight(words, scales):
    g, p, n, _ = words.shape
    vals = np.ascontiguousarray(words).view(ml_dtypes.float8_e4m3fn).astype(np.float64) * np.repeat(np.exp2(scales.astype(np.float64) - 127.0), 8, axis=1)[..., None]
    return vals.transpose(0, 1, 3, 2).reshape(g * 512, n)


E2M1 = np.array([0.0, 0.5, 1.0, 1.5, 2.0, 3.0, 4.0, 6.0, -0.0, -0.5, -1.0, -1.5, -2.0, -3.0, -4.0, -6.0])


def pack_fp4(w):
    k, n = w.shape
    w = f64(np.asarray(w, np.float32).astype(ml_dtypes.bfloat16)).reshape(k // 32, 32, n)
    amax = np.abs(w).max(1)
    mant, ex = np.frexp(amax / 6.0)
    byte = np.clip(np.where(amax > 0, np.where(mant > 0.5, ex, ex - 1) + 127, 1), 1, 254)
    scaled = (w * np.exp2(127.0 - byte)[:, None, :]).reshape(k, n).astype(np.float32)
    c = np.ascontiguousarray(scaled.reshape(k // 512, 128, 4, n).transpose(0, 1, 3, 2)).astype(ml_dtypes.float4_e2m1fn).view(np.uint8) & 0xF
    words = (c[..., 0::2] | (c[..., 1::2] << 4)).reshape(k // 512, 128, 2 * n)
    return np.ascontiguousarray(words), np.ascontiguousarray(byte.astype(np.uint8).reshape(k // 512, 16, n))


def unpack_fp4(words, scales):
    g, _, n = scales.shape
    words = np.ascontiguousarray(words).reshape(g, 128, n, 2)
    nib = np.empty((g, 128, n, 4), np.uint8)
    nib[..., 0::2] = words & 0xF
    nib[..., 1::2] = words >> 4
    vals = E2M1[nib] * np.repeat(np.exp2(scales.astype(np.float64) - 127.0), 8, axis=1)[..., None]
    return vals.transpose(0, 1, 3, 2).reshape(g * 512, n)


def relu(v):
    return np.maximum(v, 0.0)

def planes(y):
    n, m = y.shape
    v = y.astype(np.float32).astype(ml_dtypes.bfloat16).astype(np.float64).reshape(n // 32, 32, m)
    top = np.abs(v).max(1)
    byte = np.clip(np.where(top > 0, np.frexp(top)[1] - 1 + 127 - 7, 1), 1, 254)
    codes = (v * np.exp2(127.0 - byte)[:, None, :]).reshape(n, m).astype(np.float32).astype(ml_dtypes.float8_e4m3fn).view(np.uint8)
    words = codes.reshape(n // 512, 128, 4, m).transpose(0, 1, 3, 2)
    return np.ascontiguousarray(words), np.ascontiguousarray(byte.astype(np.uint8).reshape(n // 512, 16, m))


K, T, S, N, H, W = 512, 2048, 512, 512, 512, 2048


def setup_inputs():
    n = np.random.standard_normal
    s = mx_kscale(K)[:, None]
    u = mx_kscale(H)
    packed_xT = pack_weight(n((K, T)) * s)
    packed_w1 = pack_fp4(n((K, H)) / np.sqrt(K) / s)
    packed_w2 = pack_fp4(n((H, N)) / np.sqrt(2 * H) / u[:, None])
    packed_w3 = pack_fp4(n((K, N)) / np.sqrt(2 * K) / s)
    return {
        "x_words": packed_xT[0],
        "x_scales": packed_xT[1],
        "w1_words": packed_w1[0],
        "w1_scales": packed_w1[1],
        "gn": (np.random.uniform(0.5, 1.5, (H, 1)) * u[:, None]).astype(np.float32),
        "w2_words": packed_w2[0],
        "w2_scales": packed_w2[1],
        "w3_words": packed_w3[0],
        "w3_scales": packed_w3[1],
        "offs": striped(np.random.permutation(T)[:S]),
        "n1": striped(np.random.randint(0, S, W)),
        "two": striped(np.random.permutation(T)[:S]),
        "n2": striped8(np.stack([np.random.permutation(S) for _ in range(8)])),
        "n3": striped8(np.stack([np.random.permutation(S) for _ in range(8)])),
    }


def reference(x_words, x_scales, w1_words, w1_scales, gn, w2_words, w2_scales, w3_words, w3_scales, offs, n1, two, n2, n3):
    xq = unpack_weight(x_words, x_scales)[:, unstriped(offs)]
    y = unpack_fp4(w1_words, w1_scales).T @ xq
    ex = np.exp(0.5 * y)
    mb = ex[:, unstriped(n1)]
    ms = mb.reshape(H, S, 4).sum(axis=2)
    z = f64(gn) * ((4.0 * ex) / (ms + 0.5))
    x_two = unpack_weight(x_words, x_scales)[:, unstriped(two)]
    h = unpack_fp4(w2_words, w2_scales).T @ mxq(z, 0, "e4m3") + unpack_fp4(w3_words, w3_scales).T @ x_two
    out_0 = relu(h - (h[np.arange(N)[:, None], runs(n2, N)])) + 0.5 * (relu(h[np.arange(N)[:, None], runs(n3, N)] - h))
    return (out_0,) + planes(out_0)

@@ -1,0 +1,292 @@
+from contextlib import ExitStack
+
+import concourse.mybir as mybir
+from concourse.masks import make_identity
+
+K, T, S, N, H, W = 512, 2048, 512, 512, 512, 2048
+FLOPS = 2 * 3 * 512 * 512 * 512
+
+F32 = mybir.dt.float32
+BF16 = mybir.dt.bfloat16
+I32 = mybir.dt.int32
+U32 = mybir.dt.uint32
+U16 = mybir.dt.uint16
+U8 = mybir.dt.uint8
+FP8X4 = mybir.dt.float8_e4m3fn_x4
+FP4X4 = mybir.dt.float4_e2m1fn_x4
+ALU = mybir.AluOpType
+ACT = mybir.ActivationFunctionType
+
+P = 128
+PACK = 4
+BLK = 128
+NBLK = S // BLK
+SPARE = 16
+PE_BLOCKS = (0, 1, 2)
+V_GATHERS = ((0, 0), (0, 1), (1, 0), (1, 1), (2, 0), (3, 0))
+CHUNKS = (128, 128, 128, 128)
+V_GATHERS2 = ((0, 1, 0), (0, 1, 1), (0, 3, 0), (0, 3, 1))
+S_WOVEN = (0, 1, 2)
+
+
+def tile_picked_mixingsharehinge_none_po_kernel(
+    tc, x_words, x_scales, w1_words, w1_scales, gn, w2_words, w2_scales, w3_words, w3_scales,
+    offs, n1, two, n2, n3, out_0, out_1, out_2,
+):
+    nc = tc.nc
+    with ExitStack() as ctx:
+        keep = ctx.enter_context(tc.tile_pool(name="keep", bufs=1))
+        ring = ctx.enter_context(tc.tile_pool(name="ring", bufs=2))
+        psum = ctx.enter_context(tc.psum_pool(name="psum", bufs=1))
+
+        def held(shape, dtype, name):
+            return keep.tile(shape, dtype, name=name, align_bytes=64)
+
+        def load_list(src, name):
+            tile = held(list(src.shape), U16, name)
+            nc.sync.dma_start(tile[:], src)
+            return tile
+
+        def scale_tile(width, name, engine):
+            tile = held([P, width], U8, name)
+            engine.memset(tile[:].bitcast(I32), 0)
+            return tile
+
+        def load_scales(tile, src, queues):
+            rows = src[0].bitcast(I32)
+            for q in range(4):
+                queues[q].dma_start(tile[32 * q : 32 * q + 4, :].bitcast(I32), rows[4 * q : 4 * q + 4, :])
+
+        def load_words(src, name):
+            tile = keep.tile([P, 2 * N], U8, name=name, align_bytes=64)
+            nc.sync.dma_start(tile[:].bitcast(I32), src[0].bitcast(I32))
+            return tile
+
+        def deal(words, scales, name):
+            dw = held([P, 2 * N], U8, name + "_dw")
+            ds = held([P, N], U8, name + "_ds")
+            nc.vector.tensor_copy(
+                dw[:].rearrange("p (t m b) -> p t m b", t=PACK, b=2),
+                words[:].rearrange("p (m t b) -> p t m b", t=PACK, b=2),
+            )
+            nc.vector.tensor_copy(
+                ds[:].rearrange("p (t m) -> p t m", t=PACK),
+                scales[:].rearrange("p (m t) -> p t m", t=PACK),
+            )
+            return dw, ds
+
+        def stationary(dealt, t):
+            dw, ds = dealt
+            return dict(
+                lhsT=dw[:, 2 * P * t : 2 * P * (t + 1)].bitcast(FP4X4),
+                lhsT_scale=ds[:, P * t : P * (t + 1)],
+            )
+
+        def gather(on_vector, out, window, offsets):
+            if on_vector:
+                nc.vector.tensor_copy(out, window[:].indirect(offsets))
+            else:
+                nc.scalar.activation(out, window[:].indirect(offsets), ACT.Copy)
+
+        xs = scale_tile(T, "xs", nc.vector)
+        w1s = scale_tile(H, "w1s", nc.vector)
+        w3s = scale_tile(N, "w3s", nc.gpsimd)
+        w2s = scale_tile(N, "w2s", nc.gpsimd)
+        ex = [held([P, S + SPARE], F32, "ex%d" % t) for t in range(PACK)]
+        for t in range(PACK):
+            nc.gpsimd.memset(ex[t][:, S:], 0.0)
+
+        xw = held([P, T], U32, "xw")
+        gn_sb = held([P, PACK], F32, "gn_sb")
+        offs_sb = load_list(offs, "offs_sb")
+        w1w = load_words(w1_words, "w1w")
+        nc.scalar.dma_start(gn_sb[:], gn.rearrange("(p t) o -> p (t o)", t=PACK))
+        nc.sync.dma_start(xw[:].bitcast(I32), x_words[0].rearrange("p n r -> p (n r)").bitcast(I32))
+        load_scales(xs, x_scales, [nc.sync] * 4)
+        load_scales(w1s, w1_scales, [nc.sync] * 4)
+        n1_sb = load_list(n1, "n1_sb")
+        w3w = load_words(w3_words, "w3w")
+        load_scales(w3s, w3_scales, [nc.sync] * 4)
+        two_sb = load_list(two, "two_sb")
+        w2w = load_words(w2_words, "w2w")
+        load_scales(w2s, w2_scales, [nc.sync] * 4)
+        n2_sb = load_list(n2, "n2_sb")
+        n3_sb = load_list(n3, "n3_sb")
+
+        g4 = held([P, PACK], F32, "g4")
+        nc.scalar.activation(g4[:], gn_sb[:], ACT.Copy, scale=4.0)
+        ident = held([P, P], F32, "ident")
+        make_identity(nc, ident[:])
+
+        def pick(lst, name):
+            words = keep.tile([P, S], U32, name=name + "_w", tag="picked_w", align_bytes=64)
+            scales = keep.tile([P, S], U8, name=name + "_s", tag="picked_s", align_bytes=64)
+            nc.vector.tensor_copy(scales[:], xs[:].indirect(lst[:]))
+            nc.vector.tensor_copy(words[:], xw[:].indirect(lst[:]))
+            return words, scales
+
+        w1d = deal(w1w, w1s, "w1")
+        xa_w, xa_s = pick(offs_sb, "xa")
+        for t in range(PACK):
+            y = psum.tile([P, S], F32, name="y%d" % t, tag="bank%d" % t)
+            nc.tensor.matmul_mx(
+                out=y[:], rhs=xa_w[:].bitcast(FP8X4), rhs_scale=xa_s[:], start=True, stop=True, **stationary(w1d, t)
+            )
+            nc.scalar.activation(ex[t][:, :S], y[:], ACT.Exp, scale=0.5)
+
+        h = {}
+
+        def fetch(b, t, out):
+            cols = PACK * BLK // 16
+            gather((b, t) in V_GATHERS, out, ex[t], n1_sb[:, cols * b : cols * (b + 1)])
+
+        def sums_pe(b, mb):
+            turned = psum.tile([P, PACK, P], F32, name="turned", tag="bank%d" % (4 + b))
+            for t in range(PACK):
+                for c in range(PACK):
+                    nc.tensor.matmul(
+                        turned[:, t, :], lhsT=mb[:, t, c :: PACK], rhs=ident[:],
+                        start=(c == 0), stop=(c == PACK - 1), is_transpose=True,
+                    )
+            return turned
+
+        def root_pe(b, turned):
+            root_t = ring.tile([P, PACK, P], F32, name="root_t")
+            nc.scalar.activation(root_t[:], turned[:], ACT.Abs_reciprocal_sqrt, bias=0.5)
+            root = psum.tile([P, PACK, BLK], F32, name="root", tag="bank%d" % (6 + b))
+            for t in range(PACK):
+                nc.tensor.transpose(root[:, t, :], root_t[:, t, :], ident[:])
+            return root
+
+        def sums_vector(mb, ms, tag):
+            pairs = keep.tile([P, mb.shape[1], BLK, 2], F32, name="pairs", tag=tag)
+            quads = mb.rearrange("p t (j c) -> p t j c", c=PACK)
+            nc.vector.tensor_tensor(pairs[:], quads[:, :, :, 0:2], quads[:, :, :, 2:4], ALU.add)
+            nc.vector.tensor_tensor(ms, pairs[:, :, :, 0], pairs[:, :, :, 1], ALU.add)
+
+        def root_sb(ms, root, ts):
+            nc.scalar.activation(root[:, ts], ms[:, ts], ACT.Abs_reciprocal_sqrt, bias=0.5)
+
+        def second_layer(b, root, w2d):
+            cols = slice(BLK * b, BLK * (b + 1))
+            h[b] = psum.tile([P, PACK, BLK], F32, name="h", tag="bank%d" % (4 + b))
+            for t in range(PACK):
+                nc.tensor.matmul_mx(
+                    out=h[b][:, t, :], rhs=xb_w[:, cols].bitcast(FP8X4), rhs_scale=xb_s[:, cols],
+                    start=(t == 0), stop=False, **stationary(w3d, t)
+                )
+            u = ring.tile([P, PACK, BLK], F32, name="u")
+            for t in range(PACK):
+                nc.vector.scalar_tensor_tensor(u[:, t, :], ex[t][:, cols], g4[:, t : t + 1], root[:, t, :], ALU.mult, ALU.mult)
+            z = ring.tile([P, BLK, PACK], BF16, name="z", align_bytes=64)
+            nc.vector.tensor_tensor(
+                z[:].rearrange("p (c i) t -> p c t i", i=4),
+                u[:].rearrange("p t (c i) -> p c t i", i=4),
+                root[:].rearrange("p t (c i) -> p c t i", i=4),
+                ALU.mult,
+            )
+            zw = ring.tile([P, BLK], U32, name="zw", align_bytes=64)
+            zs = ring.tile([P, BLK], U8, name="zs", align_bytes=64)
+            nc.vector.quantize_mx(zw[:].bitcast(FP8X4), zs[:], z[:].rearrange("p j t -> p (j t)"))
+            for t in range(PACK):
+                nc.tensor.matmul_mx(
+                    out=h[b][:, t, :], rhs=zw[:].bitcast(FP8X4), rhs_scale=zs[:],
+                    start=False, stop=(t == PACK - 1), **stationary(w2d, t)
+                )
+
+        mb = [held([P, PACK, PACK * BLK], F32, "mb%d" % b) for b in range(NBLK)]
+        for t in range(PACK):
+            fetch(0, t, mb[0][:, t, :])
+        turned0 = sums_pe(0, mb[0])
+        for t in range(PACK):
+            fetch(1, t, mb[1][:, t, :])
+        turned1 = sums_pe(1, mb[1])
+        fetch(2, 1, mb[2][:, 1, :])
+        root0 = root_pe(0, turned0)
+        w3d = deal(w3w, w3s, "w3")
+        xb_w, xb_s = pick(two_sb, "xb")
+        w2d = deal(w2w, w2s, "w2")
+        ms2 = held([P, PACK, BLK], F32, "ms2")
+        root2 = held([P, PACK, BLK], F32, "root2")
+        ms3 = held([P, PACK, BLK], F32, "ms3")
+        root3 = held([P, PACK, BLK], F32, "root3")
+        fetch(2, 0, mb[2][:, 0, :])
+        fetch(3, 0, mb[3][:, 0, :])
+        fetch(2, 2, mb[2][:, 2, :])
+        root1 = root_pe(1, turned1)
+        second_layer(0, root0, w2d)
+        fetch(2, 3, mb[2][:, 3, :])
+        sums_vector(mb[2][:, 0:2], ms2[:, 0:2], "pairs_a")
+        second_layer(1, root1, w2d)
+        sums_vector(mb[2][:, 2:4], ms2[:, 2:4], "pairs_b")
+        fetch(3, 1, mb[3][:, 1, :])
+        fetch(3, 2, mb[3][:, 2, :])
+        root_sb(ms2, root2, slice(0, 4))
+        last = keep.tile([P, 1, PACK * BLK], F32, name="last", tag="pairs_b")
+        fetch(3, 3, last[:, 0, :])
+        sums_vector(mb[3][:, 0:3], ms3[:, 0:3], "pairs_c")
+        root_sb(ms3, root3, slice(0, 3))
+        second_layer(2, root2, w2d)
+        sums_vector(last[:], ms3[:, 3:4], "pairs_a")
+        root_sb(ms3, root3, slice(3, 4))
+        second_layer(3, root3, w2d)
+
+        half = [held([P, S], F32, "half%d" % t) for t in range(PACK)]
+        for b in range(NBLK):
+            cols = slice(BLK * b, BLK * (b + 1))
+            for t in range(PACK):
+                if b == NBLK - 1 and t % 2:
+                    nc.vector.tensor_scalar(half[t][:, cols], h[b][:, t, :], 0.5, None, ALU.mult)
+                else:
+                    nc.scalar.activation(half[t][:, cols], h[b][:, t, :], ACT.Copy, scale=0.5)
+
+        ow = held([P, S], U32, "ow")
+        osc = held([P, S], U8, "osc")
+        out_rows = out_0.rearrange("(p t) j -> p t j", t=PACK)
+        out_words = out_1[0].rearrange("p j r -> p (j r)").bitcast(I32)
+        starts = [sum(CHUNKS[:ci]) for ci in range(len(CHUNKS))]
+
+        def hinge(ci):
+            width = CHUNKS[ci]
+            cols = slice(starts[ci], starts[ci] + width)
+            lcols = slice(starts[ci] // 16, (starts[ci] + width) // 16)
+            got = ring.tile([P, PACK, 2, width], F32, name="got", bufs=4)
+            diff = ring.tile([P, PACK, 2, width], F32, name="diff")
+            down = ring.tile([P, PACK, width], F32, name="down")
+            res = held([P, PACK, width], F32, "res%d" % ci)
+            groups = (slice(0, 3), slice(3, 4)) if ci == len(CHUNKS) - 1 else (slice(0, 4),)
+            for ts in groups:
+                for t in range(ts.start, ts.stop):
+                    gather((ci, t, 0) in V_GATHERS2, got[:, t, 0, :], half[t], n2_sb[:, lcols])
+                    gather((ci, t, 1) in V_GATHERS2, got[:, t, 1, :], half[t], n3_sb[:, lcols])
+                    nc.vector.tensor_tensor(
+                        diff[:, t], got[:, t], half[t][:, cols].unsqueeze(1).to_broadcast([P, 2, width]), ALU.subtract
+                    )
+                nc.vector.tensor_scalar(down[:, ts], diff[:, ts, 0, :], 0.0, -2.0, ALU.min, ALU.mult)
+                nc.vector.scalar_tensor_tensor(res[:, ts], diff[:, ts, 1, :], 0.0, down[:, ts], ALU.max, ALU.add)
+            nc.sync.dma_start(out_rows[:, :, cols], res[:])
+            return res
+
+        woven = held([P, S, PACK], BF16, "woven")
+
+        def weave(ci, res):
+            cols = slice(starts[ci], starts[ci] + CHUNKS[ci])
+            move = nc.scalar.copy if ci in S_WOVEN else nc.vector.tensor_copy
+            move(
+                woven[:, cols].rearrange("p (c i) t -> p c t i", i=4),
+                res[:].rearrange("p t (c i) -> p c t i", i=4),
+            )
+
+        def planes(cols):
+            nc.vector.quantize_mx(ow[:, cols].bitcast(FP8X4), osc[:, cols], woven[:, cols].rearrange("p j t -> p (j t)"))
+            nc.sync.dma_start(out_words[:, cols], ow[:, cols].bitcast(I32))
+
+        results = [hinge(ci) for ci in range(len(CHUNKS))]
+        for ci in range(len(CHUNKS)):
+            weave(ci, results[ci])
+        for cols in (slice(0, 256), slice(256, 512)):
+            planes(cols)
+        scale_rows = out_2[0].bitcast(I32)
+        for q in range(4):
+            queue = nc.scalar if q % 2 else nc.sync
+            queue.dma_start(scale_rows[4 * q : 4 * q + 4, :], osc[32 * q : 32 * q + 4, :].bitcast(I32))

@@ -22,10 +22,14 @@ PACK = 4
 BLK = 128
 NBLK = S // BLK
 SPARE = 16
+TURNED_BANK = (4, 5, 4)
+ROOT_BANK = (6, 7, 0)
+H_BANK = (6, 7, 0, 5)
+S_RELU = ()
 PE_BLOCKS = (0, 1, 2)
-V_GATHERS = ((0, 0), (0, 1), (1, 0), (1, 1), (2, 0), (3, 0))
+V_GATHERS = ((0, 0), (0, 1), (1, 0), (1, 1), (2, 0), (2, 1), (3, 0))
 CHUNKS = (128, 128, 128, 128)
-V_GATHERS2 = ((0, 1, 0), (0, 1, 1), (0, 3, 0), (0, 3, 1))
+V_GATHERS2 = ((0, 1, 1), (0, 3, 1), (0, 1, 0), (0, 3, 0), (1, 1, 1), (1, 3, 1))
 S_WOVEN = (0, 1, 2)
 
 
@@ -88,7 +92,7 @@ def tile_picked_mixingsharehinge_none_po_kernel(
             else:
                 nc.scalar.activation(out, window[:].indirect(offsets), ACT.Copy)
 
-        xs = scale_tile(T, "xs", nc.vector)
+        xs = scale_tile(T, "xs", nc.gpsimd)
         w1s = scale_tile(H, "w1s", nc.vector)
         w3s = scale_tile(N, "w3s", nc.gpsimd)
         w2s = scale_tile(N, "w2s", nc.gpsimd)
@@ -100,12 +104,12 @@ def tile_picked_mixingsharehinge_none_po_kernel(
         gn_sb = held([P, PACK], F32, "gn_sb")
         offs_sb = load_list(offs, "offs_sb")
         w1w = load_words(w1_words, "w1w")
-        nc.scalar.dma_start(gn_sb[:], gn.rearrange("(p t) o -> p (t o)", t=PACK))
-        nc.sync.dma_start(xw[:].bitcast(I32), x_words[0].rearrange("p n r -> p (n r)").bitcast(I32))
-        load_scales(xs, x_scales, [nc.sync] * 4)
-        load_scales(w1s, w1_scales, [nc.sync] * 4)
-        n1_sb = load_list(n1, "n1_sb")
         w3w = load_words(w3_words, "w3w")
+        load_scales(xs, x_scales, [nc.sync] * 4)
+        nc.sync.dma_start(xw[:].bitcast(I32), x_words[0].rearrange("p n r -> p (n r)").bitcast(I32))
+        load_scales(w1s, w1_scales, [nc.sync] * 4)
+        nc.sync.dma_start(gn_sb[:], gn.rearrange("(p t) o -> p (t o)", t=PACK))
+        n1_sb = load_list(n1, "n1_sb")
         load_scales(w3s, w3_scales, [nc.sync] * 4)
         two_sb = load_list(two, "two_sb")
         w2w = load_words(w2_words, "w2w")
@@ -141,7 +145,7 @@ def tile_picked_mixingsharehinge_none_po_kernel(
             gather((b, t) in V_GATHERS, out, ex[t], n1_sb[:, cols * b : cols * (b + 1)])
 
         def sums_pe(b, mb):
-            turned = psum.tile([P, PACK, P], F32, name="turned", tag="bank%d" % (4 + b))
+            turned = psum.tile([P, PACK, P], F32, name="turned", tag="bank%d" % TURNED_BANK[b])
             for t in range(PACK):
                 for c in range(PACK):
                     nc.tensor.matmul(
@@ -153,7 +157,7 @@ def tile_picked_mixingsharehinge_none_po_kernel(
         def root_pe(b, turned):
             root_t = ring.tile([P, PACK, P], F32, name="root_t")
             nc.scalar.activation(root_t[:], turned[:], ACT.Abs_reciprocal_sqrt, bias=0.5)
-            root = psum.tile([P, PACK, BLK], F32, name="root", tag="bank%d" % (6 + b))
+            root = psum.tile([P, PACK, BLK], F32, name="root", tag="bank%d" % ROOT_BANK[b])
             for t in range(PACK):
                 nc.tensor.transpose(root[:, t, :], root_t[:, t, :], ident[:])
             return root
@@ -169,7 +173,7 @@ def tile_picked_mixingsharehinge_none_po_kernel(
 
         def second_layer(b, root, w2d):
             cols = slice(BLK * b, BLK * (b + 1))
-            h[b] = psum.tile([P, PACK, BLK], F32, name="h", tag="bank%d" % (4 + b))
+            h[b] = psum.tile([P, PACK, BLK], F32, name="h", tag="bank%d" % H_BANK[b])
             for t in range(PACK):
                 nc.tensor.matmul_mx(
                     out=h[b][:, t, :], rhs=xb_w[:, cols].bitcast(FP8X4), rhs_scale=xb_s[:, cols],
@@ -201,33 +205,30 @@ def tile_picked_mixingsharehinge_none_po_kernel(
         for t in range(PACK):
             fetch(1, t, mb[1][:, t, :])
         turned1 = sums_pe(1, mb[1])
-        fetch(2, 1, mb[2][:, 1, :])
+        fetch(2, 2, mb[2][:, 2, :])
         root0 = root_pe(0, turned0)
+        fetch(2, 0, mb[2][:, 0, :])
+        fetch(2, 1, mb[2][:, 1, :])
         w3d = deal(w3w, w3s, "w3")
         xb_w, xb_s = pick(two_sb, "xb")
         w2d = deal(w2w, w2s, "w2")
-        ms2 = held([P, PACK, BLK], F32, "ms2")
-        root2 = held([P, PACK, BLK], F32, "root2")
         ms3 = held([P, PACK, BLK], F32, "ms3")
         root3 = held([P, PACK, BLK], F32, "root3")
-        fetch(2, 0, mb[2][:, 0, :])
         fetch(3, 0, mb[3][:, 0, :])
-        fetch(2, 2, mb[2][:, 2, :])
-        root1 = root_pe(1, turned1)
-        second_layer(0, root0, w2d)
         fetch(2, 3, mb[2][:, 3, :])
-        sums_vector(mb[2][:, 0:2], ms2[:, 0:2], "pairs_a")
-        second_layer(1, root1, w2d)
-        sums_vector(mb[2][:, 2:4], ms2[:, 2:4], "pairs_b")
+        root1 = root_pe(1, turned1)
+        turned2 = sums_pe(2, mb[2])
+        second_layer(0, root0, w2d)
         fetch(3, 1, mb[3][:, 1, :])
         fetch(3, 2, mb[3][:, 2, :])
-        root_sb(ms2, root2, slice(0, 4))
-        last = keep.tile([P, 1, PACK * BLK], F32, name="last", tag="pairs_b")
-        fetch(3, 3, last[:, 0, :])
+        second_layer(1, root1, w2d)
+
+        fetch(3, 3, mb[3][:, 3, :])
+        root2 = root_pe(2, turned2)
         sums_vector(mb[3][:, 0:3], ms3[:, 0:3], "pairs_c")
         root_sb(ms3, root3, slice(0, 3))
+        sums_vector(mb[3][:, 3:4], ms3[:, 3:4], "pairs_a")
         second_layer(2, root2, w2d)
-        sums_vector(last[:], ms3[:, 3:4], "pairs_a")
         root_sb(ms3, root3, slice(3, 4))
         second_layer(3, root3, w2d)
 
@@ -247,23 +248,25 @@ def tile_picked_mixingsharehinge_none_po_kernel(
         starts = [sum(CHUNKS[:ci]) for ci in range(len(CHUNKS))]
 
         def hinge(ci):
-            width = CHUNKS[ci]
-            cols = slice(starts[ci], starts[ci] + width)
-            lcols = slice(starts[ci] // 16, (starts[ci] + width) // 16)
-            got = ring.tile([P, PACK, 2, width], F32, name="got", bufs=4)
-            diff = ring.tile([P, PACK, 2, width], F32, name="diff")
-            down = ring.tile([P, PACK, width], F32, name="down")
-            res = held([P, PACK, width], F32, "res%d" % ci)
-            groups = (slice(0, 3), slice(3, 4)) if ci == len(CHUNKS) - 1 else (slice(0, 4),)
-            for ts in groups:
-                for t in range(ts.start, ts.stop):
-                    gather((ci, t, 0) in V_GATHERS2, got[:, t, 0, :], half[t], n2_sb[:, lcols])
-                    gather((ci, t, 1) in V_GATHERS2, got[:, t, 1, :], half[t], n3_sb[:, lcols])
-                    nc.vector.tensor_tensor(
-                        diff[:, t], got[:, t], half[t][:, cols].unsqueeze(1).to_broadcast([P, 2, width]), ALU.subtract
-                    )
-                nc.vector.tensor_scalar(down[:, ts], diff[:, ts, 0, :], 0.0, -2.0, ALU.min, ALU.mult)
-                nc.vector.scalar_tensor_tensor(res[:, ts], diff[:, ts, 1, :], 0.0, down[:, ts], ALU.max, ALU.add)
+            cols = slice(BLK * ci, BLK * (ci + 1))
+            lcols = slice(BLK * ci // 16, BLK * (ci + 1) // 16)
+            got = held([P, 2, PACK, BLK], F32, "got%d" % ci)
+            above = ring.tile([P, PACK, BLK], F32, name="above")
+            below = ring.tile([P, PACK, BLK], F32, name="below")
+            part = ring.tile([P, PACK, BLK], F32, name="part")
+            res = held([P, PACK, BLK], F32, "res%d" % ci)
+            for side in (1, 0):
+                for t in range(PACK):
+                    gather((ci, t, side) in V_GATHERS2, got[:, side, t, :], half[t], (n2_sb, n3_sb)[side][:, lcols])
+            for ts in (slice(0, 4),):
+                nc.vector.scalar_tensor_tensor(below[:, ts], h[ci][:, ts], -0.5, got[:, 1, ts], ALU.mult, ALU.add)
+                if ci in S_RELU:
+                    nc.scalar.activation(part[:, ts], below[:, ts], ACT.Relu)
+                else:
+                    nc.vector.tensor_scalar(part[:, ts], below[:, ts], 0.0, None, ALU.max)
+            for ts in (slice(0, 3), slice(3, 4)) if ci == len(CHUNKS) - 1 else (slice(0, 4),):
+                nc.vector.scalar_tensor_tensor(above[:, ts], got[:, 0, ts], -2.0, h[ci][:, ts], ALU.mult, ALU.add)
+                nc.vector.scalar_tensor_tensor(res[:, ts], above[:, ts], 0.0, part[:, ts], ALU.max, ALU.add)
             nc.sync.dma_start(out_rows[:, :, cols], res[:])
             return res
 

from contextlib import ExitStack

import concourse.mybir as mybir
from concourse.masks import make_identity

K, T, S, N, H, W = 512, 2048, 512, 512, 512, 2048
FLOPS = 2 * 3 * 512 * 512 * 512

F32 = mybir.dt.float32
BF16 = mybir.dt.bfloat16
I32 = mybir.dt.int32
U32 = mybir.dt.uint32
U16 = mybir.dt.uint16
U8 = mybir.dt.uint8
FP8X4 = mybir.dt.float8_e4m3fn_x4
FP4X4 = mybir.dt.float4_e2m1fn_x4
ALU = mybir.AluOpType
ACT = mybir.ActivationFunctionType

P = 128
PACK = 4
BLK = 128
NBLK = S // BLK
SPARE = 16
TURNED_BANK = (4, 5, 4)
ROOT_BANK = (6, 7, 0)
H_BANK = (6, 7, 0, 5)
S_RELU = ()
PE_BLOCKS = (0, 1, 2)
V_GATHERS = ((0, 0), (0, 1), (1, 0), (1, 1), (2, 0), (2, 1), (3, 0))
CHUNKS = (128, 128, 128, 128)
V_GATHERS2 = ((0, 1, 1), (0, 3, 1), (0, 1, 0), (0, 3, 0), (1, 1, 1), (1, 3, 1))
S_WOVEN = (0, 1, 2)


def tile_picked_mixingsharehinge_none_po_kernel(
    tc, x_words, x_scales, w1_words, w1_scales, gn, w2_words, w2_scales, w3_words, w3_scales,
    offs, n1, two, n2, n3, out_0, out_1, out_2,
):
    nc = tc.nc
    with ExitStack() as ctx:
        keep = ctx.enter_context(tc.tile_pool(name="keep", bufs=1))
        ring = ctx.enter_context(tc.tile_pool(name="ring", bufs=2))
        psum = ctx.enter_context(tc.psum_pool(name="psum", bufs=1))

        def held(shape, dtype, name):
            return keep.tile(shape, dtype, name=name, align_bytes=64)

        def load_list(src, name):
            tile = held(list(src.shape), U16, name)
            nc.sync.dma_start(tile[:], src)
            return tile

        def scale_tile(width, name, engine):
            tile = held([P, width], U8, name)
            engine.memset(tile[:].bitcast(I32), 0)
            return tile

        def load_scales(tile, src, queues):
            rows = src[0].bitcast(I32)
            for q in range(4):
                queues[q].dma_start(tile[32 * q : 32 * q + 4, :].bitcast(I32), rows[4 * q : 4 * q + 4, :])

        def load_words(src, name):
            tile = keep.tile([P, 2 * N], U8, name=name, align_bytes=64)
            nc.sync.dma_start(tile[:].bitcast(I32), src[0].bitcast(I32))
            return tile

        def deal(words, scales, name):
            dw = held([P, 2 * N], U8, name + "_dw")
            ds = held([P, N], U8, name + "_ds")
            nc.vector.tensor_copy(
                dw[:].rearrange("p (t m b) -> p t m b", t=PACK, b=2),
                words[:].rearrange("p (m t b) -> p t m b", t=PACK, b=2),
            )
            nc.vector.tensor_copy(
                ds[:].rearrange("p (t m) -> p t m", t=PACK),
                scales[:].rearrange("p (m t) -> p t m", t=PACK),
            )
            return dw, ds

        def stationary(dealt, t):
            dw, ds = dealt
            return dict(
                lhsT=dw[:, 2 * P * t : 2 * P * (t + 1)].bitcast(FP4X4),
                lhsT_scale=ds[:, P * t : P * (t + 1)],
            )

        def gather(on_vector, out, window, offsets):
            if on_vector:
                nc.vector.tensor_copy(out, window[:].indirect(offsets))
            else:
                nc.scalar.activation(out, window[:].indirect(offsets), ACT.Copy)

        xs = scale_tile(T, "xs", nc.gpsimd)
        w1s = scale_tile(H, "w1s", nc.vector)
        w3s = scale_tile(N, "w3s", nc.gpsimd)
        w2s = scale_tile(N, "w2s", nc.gpsimd)
        ex = [held([P, S + SPARE], F32, "ex%d" % t) for t in range(PACK)]
        for t in range(PACK):
            nc.gpsimd.memset(ex[t][:, S:], 0.0)

        xw = held([P, T], U32, "xw")
        gn_sb = held([P, PACK], F32, "gn_sb")
        offs_sb = load_list(offs, "offs_sb")
        w1w = load_words(w1_words, "w1w")
        w3w = load_words(w3_words, "w3w")
        load_scales(xs, x_scales, [nc.sync] * 4)
        nc.sync.dma_start(xw[:].bitcast(I32), x_words[0].rearrange("p n r -> p (n r)").bitcast(I32))
        load_scales(w1s, w1_scales, [nc.sync] * 4)
        nc.sync.dma_start(gn_sb[:], gn.rearrange("(p t) o -> p (t o)", t=PACK))
        n1_sb = load_list(n1, "n1_sb")
        load_scales(w3s, w3_scales, [nc.sync] * 4)
        two_sb = load_list(two, "two_sb")
        w2w = load_words(w2_words, "w2w")
        load_scales(w2s, w2_scales, [nc.sync] * 4)
        n2_sb = load_list(n2, "n2_sb")
        n3_sb = load_list(n3, "n3_sb")

        g4 = held([P, PACK], F32, "g4")
        nc.scalar.activation(g4[:], gn_sb[:], ACT.Copy, scale=4.0)
        ident = held([P, P], F32, "ident")
        make_identity(nc, ident[:])

        def pick(lst, name):
            words = keep.tile([P, S], U32, name=name + "_w", tag="picked_w", align_bytes=64)
            scales = keep.tile([P, S], U8, name=name + "_s", tag="picked_s", align_bytes=64)
            nc.vector.tensor_copy(scales[:], xs[:].indirect(lst[:]))
            nc.vector.tensor_copy(words[:], xw[:].indirect(lst[:]))
            return words, scales

        w1d = deal(w1w, w1s, "w1")
        xa_w, xa_s = pick(offs_sb, "xa")
        for t in range(PACK):
            y = psum.tile([P, S], F32, name="y%d" % t, tag="bank%d" % t)
            nc.tensor.matmul_mx(
                out=y[:], rhs=xa_w[:].bitcast(FP8X4), rhs_scale=xa_s[:], start=True, stop=True, **stationary(w1d, t)
            )
            nc.scalar.activation(ex[t][:, :S], y[:], ACT.Exp, scale=0.5)

        h = {}

        def fetch(b, t, out):
            cols = PACK * BLK // 16
            gather((b, t) in V_GATHERS, out, ex[t], n1_sb[:, cols * b : cols * (b + 1)])

        def sums_pe(b, mb):
            turned = psum.tile([P, PACK, P], F32, name="turned", tag="bank%d" % TURNED_BANK[b])
            for t in range(PACK):
                for c in range(PACK):
                    nc.tensor.matmul(
                        turned[:, t, :], lhsT=mb[:, t, c :: PACK], rhs=ident[:],
                        start=(c == 0), stop=(c == PACK - 1), is_transpose=True,
                    )
            return turned

        def root_pe(b, turned):
            root_t = ring.tile([P, PACK, P], F32, name="root_t")
            nc.scalar.activation(root_t[:], turned[:], ACT.Abs_reciprocal_sqrt, bias=0.5)
            root = psum.tile([P, PACK, BLK], F32, name="root", tag="bank%d" % ROOT_BANK[b])
            for t in range(PACK):
                nc.tensor.transpose(root[:, t, :], root_t[:, t, :], ident[:])
            return root

        def sums_vector(mb, ms, tag):
            pairs = keep.tile([P, mb.shape[1], BLK, 2], F32, name="pairs", tag=tag)
            quads = mb.rearrange("p t (j c) -> p t j c", c=PACK)
            nc.vector.tensor_tensor(pairs[:], quads[:, :, :, 0:2], quads[:, :, :, 2:4], ALU.add)
            nc.vector.tensor_tensor(ms, pairs[:, :, :, 0], pairs[:, :, :, 1], ALU.add)

        def root_sb(ms, root, ts):
            nc.scalar.activation(root[:, ts], ms[:, ts], ACT.Abs_reciprocal_sqrt, bias=0.5)

        def second_layer(b, root, w2d):
            cols = slice(BLK * b, BLK * (b + 1))
            h[b] = psum.tile([P, PACK, BLK], F32, name="h", tag="bank%d" % H_BANK[b])
            for t in range(PACK):
                nc.tensor.matmul_mx(
                    out=h[b][:, t, :], rhs=xb_w[:, cols].bitcast(FP8X4), rhs_scale=xb_s[:, cols],
                    start=(t == 0), stop=False, **stationary(w3d, t)
                )
            u = ring.tile([P, PACK, BLK], F32, name="u")
            for t in range(PACK):
                nc.vector.scalar_tensor_tensor(u[:, t, :], ex[t][:, cols], g4[:, t : t + 1], root[:, t, :], ALU.mult, ALU.mult)
            z = ring.tile([P, BLK, PACK], BF16, name="z", align_bytes=64)
            nc.vector.tensor_tensor(
                z[:].rearrange("p (c i) t -> p c t i", i=4),
                u[:].rearrange("p t (c i) -> p c t i", i=4),
                root[:].rearrange("p t (c i) -> p c t i", i=4),
                ALU.mult,
            )
            zw = ring.tile([P, BLK], U32, name="zw", align_bytes=64)
            zs = ring.tile([P, BLK], U8, name="zs", align_bytes=64)
            nc.vector.quantize_mx(zw[:].bitcast(FP8X4), zs[:], z[:].rearrange("p j t -> p (j t)"))
            for t in range(PACK):
                nc.tensor.matmul_mx(
                    out=h[b][:, t, :], rhs=zw[:].bitcast(FP8X4), rhs_scale=zs[:],
                    start=False, stop=(t == PACK - 1), **stationary(w2d, t)
                )

        mb = [held([P, PACK, PACK * BLK], F32, "mb%d" % b) for b in range(NBLK)]
        for t in range(PACK):
            fetch(0, t, mb[0][:, t, :])
        turned0 = sums_pe(0, mb[0])
        for t in range(PACK):
            fetch(1, t, mb[1][:, t, :])
        turned1 = sums_pe(1, mb[1])
        fetch(2, 2, mb[2][:, 2, :])
        root0 = root_pe(0, turned0)
        fetch(2, 0, mb[2][:, 0, :])
        fetch(2, 1, mb[2][:, 1, :])
        w3d = deal(w3w, w3s, "w3")
        xb_w, xb_s = pick(two_sb, "xb")
        w2d = deal(w2w, w2s, "w2")
        ms3 = held([P, PACK, BLK], F32, "ms3")
        root3 = held([P, PACK, BLK], F32, "root3")
        fetch(3, 0, mb[3][:, 0, :])
        fetch(2, 3, mb[2][:, 3, :])
        root1 = root_pe(1, turned1)
        turned2 = sums_pe(2, mb[2])
        second_layer(0, root0, w2d)
        fetch(3, 1, mb[3][:, 1, :])
        fetch(3, 2, mb[3][:, 2, :])
        second_layer(1, root1, w2d)

        fetch(3, 3, mb[3][:, 3, :])
        root2 = root_pe(2, turned2)
        sums_vector(mb[3][:, 0:3], ms3[:, 0:3], "pairs_c")
        root_sb(ms3, root3, slice(0, 3))
        sums_vector(mb[3][:, 3:4], ms3[:, 3:4], "pairs_a")
        second_layer(2, root2, w2d)
        root_sb(ms3, root3, slice(3, 4))
        second_layer(3, root3, w2d)

        half = [held([P, S], F32, "half%d" % t) for t in range(PACK)]
        for b in range(NBLK):
            cols = slice(BLK * b, BLK * (b + 1))
            for t in range(PACK):
                if b == NBLK - 1 and t % 2:
                    nc.vector.tensor_scalar(half[t][:, cols], h[b][:, t, :], 0.5, None, ALU.mult)
                else:
                    nc.scalar.activation(half[t][:, cols], h[b][:, t, :], ACT.Copy, scale=0.5)

        ow = held([P, S], U32, "ow")
        osc = held([P, S], U8, "osc")
        out_rows = out_0.rearrange("(p t) j -> p t j", t=PACK)
        out_words = out_1[0].rearrange("p j r -> p (j r)").bitcast(I32)
        starts = [sum(CHUNKS[:ci]) for ci in range(len(CHUNKS))]

        def hinge(ci):
            cols = slice(BLK * ci, BLK * (ci + 1))
            lcols = slice(BLK * ci // 16, BLK * (ci + 1) // 16)
            got = held([P, 2, PACK, BLK], F32, "got%d" % ci)
            above = ring.tile([P, PACK, BLK], F32, name="above")
            below = ring.tile([P, PACK, BLK], F32, name="below")
            part = ring.tile([P, PACK, BLK], F32, name="part")
            res = held([P, PACK, BLK], F32, "res%d" % ci)
            for side in (1, 0):
                for t in range(PACK):
                    gather((ci, t, side) in V_GATHERS2, got[:, side, t, :], half[t], (n2_sb, n3_sb)[side][:, lcols])
            for ts in (slice(0, 4),):
                nc.vector.scalar_tensor_tensor(below[:, ts], h[ci][:, ts], -0.5, got[:, 1, ts], ALU.mult, ALU.add)
                if ci in S_RELU:
                    nc.scalar.activation(part[:, ts], below[:, ts], ACT.Relu)
                else:
                    nc.vector.tensor_scalar(part[:, ts], below[:, ts], 0.0, None, ALU.max)
            for ts in (slice(0, 3), slice(3, 4)) if ci == len(CHUNKS) - 1 else (slice(0, 4),):
                nc.vector.scalar_tensor_tensor(above[:, ts], got[:, 0, ts], -2.0, h[ci][:, ts], ALU.mult, ALU.add)
                nc.vector.scalar_tensor_tensor(res[:, ts], above[:, ts], 0.0, part[:, ts], ALU.max, ALU.add)
            nc.sync.dma_start(out_rows[:, :, cols], res[:])
            return res

        woven = held([P, S, PACK], BF16, "woven")

        def weave(ci, res):
            cols = slice(starts[ci], starts[ci] + CHUNKS[ci])
            move = nc.scalar.copy if ci in S_WOVEN else nc.vector.tensor_copy
            move(
                woven[:, cols].rearrange("p (c i) t -> p c t i", i=4),
                res[:].rearrange("p t (c i) -> p c t i", i=4),
            )

        def planes(cols):
            nc.vector.quantize_mx(ow[:, cols].bitcast(FP8X4), osc[:, cols], woven[:, cols].rearrange("p j t -> p (j t)"))
            nc.sync.dma_start(out_words[:, cols], ow[:, cols].bitcast(I32))

        results = [hinge(ci) for ci in range(len(CHUNKS))]
        for ci in range(len(CHUNKS)):
            weave(ci, results[ci])
        for cols in (slice(0, 256), slice(256, 512)):
            planes(cols)
        scale_rows = out_2[0].bitcast(I32)
        for q in range(4):
            queue = nc.scalar if q % 2 else nc.sync
            queue.dma_start(scale_rows[4 * q : 4 * q + 4, :], osc[32 * q : 32 * q + 4, :].bitcast(I32))
